import numpy as np
import ml_dtypes


def mxq(x, axis, fmt="e4m3"):
    dtype, down = {"e4m3": (ml_dtypes.float8_e4m3fn, 7), "e5m2": (ml_dtypes.float8_e5m2, 14)}[fmt]
    v = np.moveaxis(np.asarray(x, np.float32).astype(ml_dtypes.bfloat16).astype(np.float64), axis, -1)
    blocks = v.reshape(v.shape[:-1] + (-1, 32))
    amax = np.abs(blocks).max(-1, keepdims=True)
    byte = np.maximum(np.where(amax > 0, np.frexp(amax)[1] - 1 + 127, 0) - down, 1)
    scale = np.exp2(byte - 127.0)
    codes = (blocks / scale).astype(np.float32).astype(dtype).astype(np.float64)
    return np.moveaxis((codes * scale).reshape(v.shape), -1, axis)


WIDE = False


def mx_kscale(k):
    if not WIDE:
        return np.ones(k)
    levels = np.array([10, -10, 5, -5, 0])
    if k % 512:
        return np.exp2(np.random.permutation(np.resize(levels, k // 32))).repeat(32)
    a = np.empty((k // 512, 16))
    for p in range(k // 512):
        a[p, :8] = np.random.permutation(np.resize(levels, 8))
        for g in range(8):
            far = levels[np.abs(levels - a[p, g]) >= 10]
            a[p, g + 8] = far[np.random.randint(len(far))]
    return np.exp2(a.ravel()).repeat(32)


def f64(x):
    return np.asarray(x).astype(np.float64)


def striped(idx):
    return np.tile(idx.reshape(-1, 16).T, (8, 1)).astype(np.uint16)


def unstriped(offs):
    return offs[:16].T.reshape(-1).astype(np.int64)


def pack_weight(w):
    k, n = w.shape
    w = f64(np.asarray(w, np.float32).astype(ml_dtypes.bfloat16)).reshape(k // 32, 32, n)
    amax = np.abs(w).max(1)
    byte = np.clip(np.where(amax > 0, np.frexp(amax)[1] - 1 + 127 - 7, 1), 1, 254)
    scaled = (w * np.exp2(127.0 - byte)[:, None, :]).reshape(k, n).astype(np.float32)
    words = np.ascontiguousarray(scaled.reshape(k // 512, 128, 4, n).transpose(0, 1, 3, 2)).astype(ml_dtypes.float8_e4m3fn).view(np.uint8)
    return words, np.ascontiguousarray(byte.astype(np.uint8).reshape(k // 512, 16, n))


def unpack_weight(words, scales):
    g, p, n, _ = words.shape
    vals = np.ascontiguousarray(words).view(ml_dtypes.float8_e4m3fn).astype(np.float64) * np.repeat(np.exp2(scales.astype(np.float64) - 127.0), 8, axis=1)[..., None]
    return vals.transpose(0, 1, 3, 2).reshape(g * 512, n)


K, T, E, C, N = 512, 1024, 16, 128, 128


def by_expert(wq, xq):
    return np.concatenate([wq[e].T @ xq[:, e * C:(e + 1) * C] for e in range(E)], axis=1)


def setup_inputs():
    n = np.random.standard_normal
    s = mx_kscale(K)[:, None]
    first = np.random.permutation(np.repeat(np.arange(E), T // E))
    second = (first + 1 + np.random.permutation(np.repeat(np.arange(E - 1), -(-T // (E - 1)))[:T])) % E
    while np.bincount(second, minlength=E).max() != T // E:
        load = np.bincount(second, minlength=E); hi, lo = int(load.argmax()), int(load.argmin())
        t = np.flatnonzero((second == hi) & (first != lo))[0]; second[t] = lo
    slot_token = np.empty(E * C, np.int64); pos = np.empty((2, T), np.int64); fill = np.zeros(E, np.int64)
    place = np.stack([np.random.permutation(C) for _ in range(E)])
    for r, deal in enumerate((first, second)):
        for t in np.random.permutation(T):
            e = deal[t]; j = e * C + place[e, fill[e]]; fill[e] += 1; slot_token[j] = t; pos[r, t] = j
    g = np.random.uniform(0.2, 0.8, T)
    packed = [pack_weight(m) for m in n((E, K, N)) / np.sqrt(K) / s[None]]
    return {
        "xT": (n((K, T)) * s).astype(np.float32),
        "w_words": np.stack([m[0] for m in packed]),
        "w_scales": np.stack([m[1] for m in packed]),
        "gate": np.stack([np.tile(g, (N, 1)), np.tile(1.0 - g, (N, 1))]).astype(np.float32),
        "offs": striped(slot_token),
        "pos1": striped(pos[0]),
        "pos2": striped(pos[1]),
    }


def reference(xT, w_words, w_scales, gate, offs, pos1, pos2):
    idx = unstriped(offs)
    xq = mxq(f64(xT)[:, idx], 0, "e4m3")
    w = np.stack([unpack_weight(w_words[e], w_scales[e]) for e in range(E)])
    y = by_expert(w, xq)
    return f64(gate[0]) * y[:, unstriped(pos1)] + f64(gate[1]) * y[:, unstriped(pos2)]

@@ -1,0 +1,128 @@
+from contextlib import ExitStack
+
+import concourse.mybir as mybir
+
+F32 = mybir.dt.float32
+BF16 = mybir.dt.bfloat16
+I32 = mybir.dt.int32
+U32 = mybir.dt.uint32
+U16 = mybir.dt.uint16
+U8 = mybir.dt.uint8
+FP8X4 = mybir.dt.float8_e4m3fn_x4
+MULT = mybir.AluOpType.mult
+ADD = mybir.AluOpType.add
+
+P = 128
+K, T, E, C, N = 512, 1024, 16, 128, 128
+S = E * C
+FLOPS = 2 * K * N * S
+
+WIN = 2048
+CHUNKS = ((0, 256, 128), (256, 512, 128), (512, 768, 128), (768, 896, 72), (896, 1024, 88))
+
+GATHERS = (("w", 0, 1536, WIN), ("b", 0, 1536, WIN), ("w", 1536, 2048, WIN), ("b", 1536, 1920, WIN), ("b", 1920, 2048, T))
+BANKS = ((0, 4, "s"), (4, 8, "s"), (8, 12, "s"), (12, 14, "s"), (14, 15, "v"), (15, 16, "v"))
+OUT_CHUNKS = ((0, 768), (768, 1024))
+
+
+def tile_routed_moe_kernel(tc, xT, w_words, w_scales, gate, offs, pos1, pos2, out):
+    nc = tc.nc
+    with ExitStack() as ctx:
+        lists = ctx.enter_context(tc.tile_pool(name="lists", bufs=1))
+        keep = ctx.enter_context(tc.tile_pool(name="keep", bufs=1))
+        psum = ctx.enter_context(tc.psum_pool(name="psum", bufs=1))
+
+        offs_sb = lists.tile([P, S // 16], U16, name="offs_sb")
+        pos1_sb = lists.tile([P, T // 16], U16, name="pos1_sb")
+        pos2_sb = lists.tile([P, T // 16], U16, name="pos2_sb")
+
+        warm = keep.tile([P, 8], F32, name="warm")
+        warm2 = keep.tile([P, 8], F32, name="warm2")
+        nc.vector.memset(warm[:], 0.0)
+        nc.scalar.copy(out=warm2[:], in_=warm[:])
+
+        tok_words = keep.tile([P, WIN], I32, name="tok_words", align_bytes=64)
+        tok_bytes = keep.tile([P, WIN], U8, name="tok_bytes", align_bytes=64)
+        nc.vector.memset(tok_words[:, T:WIN], 0)
+        nc.vector.memset(tok_bytes[:].bitcast(I32), 0)
+        ws = keep.tile([P, E, N], U8, name="ws", align_bytes=64)
+        nc.vector.memset(ws[:].bitcast(I32), 0)
+
+        x_view = xT.rearrange("(p j) t -> p j t", j=4)
+        raws = []
+        for a, b, v in CHUNKS:
+            raw = keep.tile([P, 4, b - a], F32, name="raw%d" % a)
+            nc.sync.dma_start(out=raw[:], in_=x_view[:, :, a:b])
+            raws.append(raw)
+        nc.sync.dma_start(offs_sb[:], offs)
+
+        s_view = w_scales.rearrange("e a q n -> q (e a) n")
+        for r in range(4):
+            nc.sync.dma_start(out=ws[r:P:32, :, :].bitcast(I32), in_=s_view[r:16:4, :, :].bitcast(I32))
+        w_sb = keep.tile([P, E, N], I32, name="w_sb", align_bytes=64)
+        w_view = w_words.rearrange("e a p n r -> p (e a) (n r)").bitcast(I32)
+        for h in range(2):
+            nc.sync.dma_start(out=w_sb[:, 8 * h:8 * h + 8, :], in_=w_view[:, 8 * h:8 * h + 8, :])
+        nc.sync.dma_start(pos1_sb[:], pos1)
+        nc.sync.dma_start(pos2_sb[:], pos2)
+        gate0 = keep.tile([P, T], F32, name="gate0")
+        gate1 = keep.tile([P, T], F32, name="gate1")
+        nc.sync.dma_start(out=gate0[:], in_=gate[0])
+        nc.sync.dma_start(out=gate1[:], in_=gate[1])
+
+        for i, (a, b, v) in enumerate(CHUNKS):
+            grp = keep.tile([P, b - a, 4], BF16, name="grp%d" % a, align_bytes=64)
+            src = raws[i][:].rearrange("p j t -> p t j")
+            nc.vector.tensor_copy(out=grp[:, 0:v, :], in_=src[:, 0:v, :])
+            nc.scalar.copy(out=grp[:, v:b - a, :], in_=src[:, v:b - a, :])
+            nc.vector.quantize_mx(
+                out=tok_words[:, a:b].bitcast(FP8X4),
+                scales=tok_bytes[:, a:b],
+                in_=grp[:].rearrange("p t j -> p (t j)"),
+            )
+
+        g_words = keep.tile([P, S], U32, name="g_words", align_bytes=64)
+        g_bytes = keep.tile([P, S], U8, name="g_bytes", align_bytes=64)
+        for sort, a, b, cols in GATHERS:
+            lst = offs_sb[:, a // 16:b // 16]
+            if sort == "w":
+                nc.vector.tensor_copy(out=g_words[:, a:b], in_=tok_words[:, 0:cols].bitcast(U32).indirect(lst))
+            else:
+                nc.vector.tensor_copy(out=g_bytes[:, a:b], in_=tok_bytes[:, 0:cols].indirect(lst))
+
+        y_sb = keep.tile([P, S], F32, name="y_sb")
+        for e0, e1, eng in BANKS:
+            acc = psum.tile([P, (e1 - e0) * C], F32, name="acc%d" % e0)
+            for e in range(e0, e1):
+                nc.tensor.matmul_mx(
+                    out=acc[:, (e - e0) * C:(e - e0 + 1) * C],
+                    lhsT=w_sb[:, e, :].bitcast(FP8X4),
+                    lhsT_scale=ws[:, e, :],
+                    rhs=g_words[:, e * C:(e + 1) * C].bitcast(FP8X4),
+                    rhs_scale=g_bytes[:, e * C:(e + 1) * C],
+                    start=True,
+                    stop=True,
+                )
+            if eng == "v":
+                nc.vector.tensor_copy(out=y_sb[:, e0 * C:e1 * C], in_=acc[:])
+            else:
+                nc.scalar.copy(out=y_sb[:, e0 * C:e1 * C], in_=acc[:])
+
+        part1 = keep.tile([P, T], F32, name="part1")
+        part2 = keep.tile([P, T], F32, name="part2")
+        res = keep.tile([P, T], F32, name="res")
+
+        def fetch(part, lst, gt, a, b):
+            nc.vector.tensor_tensor(out=part[:, a:b], in0=y_sb[:].indirect(lst[:, a // 16:b // 16]), in1=gt[:, a:b], op=MULT)
+
+        def finish(a, b):
+            nc.vector.tensor_tensor(out=res[:, a:b], in0=part1[:, a:b], in1=part2[:, a:b], op=ADD)
+            nc.sync.dma_start(out=out[:, a:b], in_=res[:, a:b])
+
+        (a0, b0), (a1, b1) = OUT_CHUNKS
+        fetch(part1, pos1_sb, gate0, a0, b0)
+        fetch(part2, pos2_sb, gate1, a0, b0)
+        fetch(part1, pos1_sb, gate0, a1, b1)
+        finish(a0, b0)
+        fetch(part2, pos2_sb, gate1, a1, b1)
+        finish(a1, b1)

@@ -1,6 +1,7 @@
 from contextlib import ExitStack
 
 import concourse.mybir as mybir
+from concourse.masks import make_identity
 
 F32 = mybir.dt.float32
 BF16 = mybir.dt.bfloat16
@@ -22,7 +23,8 @@ CHUNKS = ((0, 256, 128), (256, 512, 128), (512, 768, 128), (768, 896, 72), (896,
 
 GATHERS = (("w", 0, 1536, WIN), ("b", 0, 1536, WIN), ("w", 1536, 2048, WIN), ("b", 1536, 1920, WIN), ("b", 1920, 2048, T))
 BANKS = ((0, 4, "s"), (4, 8, "s"), (8, 12, "s"), (12, 14, "s"), (14, 15, "v"), (15, 16, "v"))
-OUT_CHUNKS = ((0, 768), (768, 1024))
+PE_ADD = 384
+V_CUT = 768
 
 
 def tile_routed_moe_kernel(tc, xT, w_words, w_scales, gate, offs, pos1, pos2, out):
@@ -40,6 +42,8 @@ def tile_routed_moe_kernel(tc, xT, w_words, w_scales, gate, offs, pos1, pos2, ou
         warm2 = keep.tile([P, 8], F32, name="warm2")
         nc.vector.memset(warm[:], 0.0)
         nc.scalar.copy(out=warm2[:], in_=warm[:])
+        ident = keep.tile([P, P], F32, name="ident")
+        make_identity(nc, ident[:])
 
         tok_words = keep.tile([P, WIN], I32, name="tok_words", align_bytes=64)
         tok_bytes = keep.tile([P, WIN], U8, name="tok_bytes", align_bytes=64)
@@ -119,10 +123,15 @@ def tile_routed_moe_kernel(tc, xT, w_words, w_scales, gate, offs, pos1, pos2, ou
             nc.vector.tensor_tensor(out=res[:, a:b], in0=part1[:, a:b], in1=part2[:, a:b], op=ADD)
             nc.sync.dma_start(out=out[:, a:b], in_=res[:, a:b])
 
-        (a0, b0), (a1, b1) = OUT_CHUNKS
-        fetch(part1, pos1_sb, gate0, a0, b0)
-        fetch(part2, pos2_sb, gate1, a0, b0)
-        fetch(part1, pos1_sb, gate0, a1, b1)
-        finish(a0, b0)
-        fetch(part2, pos2_sb, gate1, a1, b1)
-        finish(a1, b1)
+        fetch(part1, pos1_sb, gate0, 0, PE_ADD)
+        fetch(part2, pos2_sb, gate1, 0, PE_ADD)
+        total = psum.tile([P, PE_ADD], F32, name="total")
+        nc.tensor.matmul(total[:], lhsT=ident[:], rhs=part1[:, 0:PE_ADD], start=True, stop=False)
+        nc.tensor.matmul(total[:], lhsT=ident[:], rhs=part2[:, 0:PE_ADD], start=False, stop=True)
+        nc.scalar.copy(out=res[:, 0:PE_ADD], in_=total[:])
+        nc.sync.dma_start(out=out[:, 0:PE_ADD], in_=res[:, 0:PE_ADD])
+        fetch(part1, pos1_sb, gate0, PE_ADD, T)
+        fetch(part2, pos2_sb, gate1, PE_ADD, V_CUT)
+        fetch(part2, pos2_sb, gate1, V_CUT, T)
+        finish(PE_ADD, V_CUT)
+        finish(V_CUT, T)

@@ -24,7 +24,8 @@ CHUNKS = ((0, 256, 128), (256, 512, 128), (512, 768, 128), (768, 896, 72), (896,
 GATHERS = (("w", 0, 1536, WIN), ("b", 0, 1536, WIN), ("w", 1536, 2048, WIN), ("b", 1536, 1920, WIN), ("b", 1920, 2048, T))
 BANKS = ((0, 4, "s"), (4, 8, "s"), (8, 12, "s"), (12, 14, "s"), (14, 15, "v"), (15, 16, "v"))
 PE_ADD = 384
-V_CUT = 768
+PE_STEP = 192
+V_CUTS = (384, 640, 896, 1024)
 
 
 def tile_routed_moe_kernel(tc, xT, w_words, w_scales, gate, offs, pos1, pos2, out):
@@ -125,13 +126,18 @@ def tile_routed_moe_kernel(tc, xT, w_words, w_scales, gate, offs, pos1, pos2, ou
 
         fetch(part1, pos1_sb, gate0, 0, PE_ADD)
         fetch(part2, pos2_sb, gate1, 0, PE_ADD)
-        total = psum.tile([P, PE_ADD], F32, name="total")
-        nc.tensor.matmul(total[:], lhsT=ident[:], rhs=part1[:, 0:PE_ADD], start=True, stop=False)
-        nc.tensor.matmul(total[:], lhsT=ident[:], rhs=part2[:, 0:PE_ADD], start=False, stop=True)
-        nc.scalar.copy(out=res[:, 0:PE_ADD], in_=total[:])
-        nc.sync.dma_start(out=out[:, 0:PE_ADD], in_=res[:, 0:PE_ADD])
-        fetch(part1, pos1_sb, gate0, PE_ADD, T)
-        fetch(part2, pos2_sb, gate1, PE_ADD, V_CUT)
-        fetch(part2, pos2_sb, gate1, V_CUT, T)
-        finish(PE_ADD, V_CUT)
-        finish(V_CUT, T)
+        for a in range(0, PE_ADD, PE_STEP):
+            b = a + PE_STEP
+            total = psum.tile([P, PE_STEP], F32, name="total%d" % a)
+            nc.tensor.matmul(total[:], lhsT=ident[:], rhs=part1[:, a:b], start=True, stop=False)
+            nc.tensor.matmul(total[:], lhsT=ident[:], rhs=part2[:, a:b], start=False, stop=True)
+            nc.scalar.copy(out=res[:, a:b], in_=total[:])
+            nc.sync.dma_start(out=out[:, a:b], in_=res[:, a:b])
+        c0, c1, c2, c3 = V_CUTS
+        fetch(part1, pos1_sb, gate0, c0, c3)
+        fetch(part2, pos2_sb, gate1, c0, c1)
+        fetch(part2, pos2_sb, gate1, c1, c2)
+        finish(c0, c1)
+        fetch(part2, pos2_sb, gate1, c2, c3)
+        finish(c1, c2)
+        finish(c2, c3)

@@ -22,7 +22,7 @@ WIN = 2048
 CHUNKS = ((0, 256, 128), (256, 512, 128), (512, 768, 128), (768, 896, 72), (896, 1024, 88))
 
 GATHERS = (("w", 0, 1536, WIN), ("b", 0, 1536, WIN), ("w", 1536, 2048, WIN), ("b", 1536, 1920, WIN), ("b", 1920, 2048, T))
-BANKS = ((0, 4, "s"), (4, 8, "s"), (8, 12, "s"), (12, 14, "s"), (14, 15, "v"), (15, 16, "v"))
+BANKS = ((0, 4, "s"), (4, 8, "s"), (8, 12, "s"), (12, 14, "s"), (14, 15, "v"), (15, 16, "s"))
 PE_ADD = 384
 PE_STEP = 192
 V_CUTS = (384, 640, 896, 1024)
@@ -132,7 +132,7 @@ def tile_routed_moe_kernel(tc, xT, w_words, w_scales, gate, offs, pos1, pos2, ou
             nc.tensor.matmul(total[:], lhsT=ident[:], rhs=part1[:, a:b], start=True, stop=False)
             nc.tensor.matmul(total[:], lhsT=ident[:], rhs=part2[:, a:b], start=False, stop=True)
             nc.scalar.copy(out=res[:, a:b], in_=total[:])
-            nc.sync.dma_start(out=out[:, a:b], in_=res[:, a:b])
+            nc.scalar.dma_start(out=out[:, a:b], in_=res[:, a:b])
         c0, c1, c2, c3 = V_CUTS
         fetch(part1, pos1_sb, gate0, c0, c3)
         fetch(part2, pos2_sb, gate1, c0, c1)

@@ -21,7 +21,7 @@ FLOPS = 2 * K * N * S
 WIN = 2048
 CHUNKS = ((0, 256, 128), (256, 512, 128), (512, 768, 128), (768, 896, 72), (896, 1024, 88))
 
-GATHERS = (("w", 0, 1536, WIN), ("b", 0, 1536, WIN), ("w", 1536, 2048, WIN), ("b", 1536, 1920, WIN), ("b", 1920, 2048, T))
+GATHERS = (("w", 0, 1536, WIN), ("b", 0, 1024, WIN), ("b", 1024, 1536, WIN), ("w", 1536, 2048, WIN), ("b", 1536, 1920, WIN), ("b", 1920, 2048, T))
 BANKS = ((0, 4, "s"), (4, 8, "s"), (8, 12, "s"), (12, 14, "s"), (14, 15, "v"), (15, 16, "s"))
 PE_ADD = 384
 PE_STEP = 192

@@ -19,7 +19,7 @@ S = E * C
 FLOPS = 2 * K * N * S
 
 WIN = 2048
-CHUNKS = ((0, 256, 128), (256, 512, 128), (512, 768, 128), (768, 896, 72), (896, 1024, 88))
+CHUNKS = ((0, 256, 160), (256, 512, 160), (512, 768, 160), (768, 896, 0), (896, 1024, 88))
 
 GATHERS = (("w", 0, 1536, WIN), ("b", 0, 1024, WIN), ("b", 1024, 1536, WIN), ("w", 1536, 2048, WIN), ("b", 1536, 1920, WIN), ("b", 1920, 2048, T))
 BANKS = ((0, 4, "s"), (4, 8, "s"), (8, 12, "s"), (12, 14, "s"), (14, 15, "v"), (15, 16, "s"))
@@ -70,15 +70,16 @@ def tile_routed_moe_kernel(tc, xT, w_words, w_scales, gate, offs, pos1, pos2, ou
             nc.sync.dma_start(out=w_sb[:, 8 * h:8 * h + 8, :], in_=w_view[:, 8 * h:8 * h + 8, :])
         nc.sync.dma_start(pos1_sb[:], pos1)
         nc.sync.dma_start(pos2_sb[:], pos2)
-        gate0 = keep.tile([P, T], F32, name="gate0")
-        gate1 = keep.tile([P, T], F32, name="gate1")
-        nc.sync.dma_start(out=gate0[:], in_=gate[0])
-        nc.sync.dma_start(out=gate1[:], in_=gate[1])
+        gates = keep.tile([P, 2, T], F32, name="gates")
+        nc.sync.dma_start(out=gates[:], in_=gate.rearrange("g p t -> p g t"))
+        gate0 = gates[:, 0, :]
+        gate1 = gates[:, 1, :]
 
         for i, (a, b, v) in enumerate(CHUNKS):
             grp = keep.tile([P, b - a, 4], BF16, name="grp%d" % a, align_bytes=64)
             src = raws[i][:].rearrange("p j t -> p t j")
-            nc.vector.tensor_copy(out=grp[:, 0:v, :], in_=src[:, 0:v, :])
+            if v:
+                nc.vector.tensor_copy(out=grp[:, 0:v, :], in_=src[:, 0:v, :])
             nc.scalar.copy(out=grp[:, v:b - a, :], in_=src[:, v:b - a, :])
             nc.vector.quantize_mx(
                 out=tok_words[:, a:b].bitcast(FP8X4),

@@ -21,8 +21,8 @@ FLOPS = 2 * K * N * S
 WIN = 2048
 CHUNKS = ((0, 256, 160), (256, 512, 160), (512, 768, 160), (768, 896, 0), (896, 1024, 88))
 
-GATHERS = (("w", 0, 1536, WIN), ("b", 0, 1024, WIN), ("b", 1024, 1536, WIN), ("w", 1536, 2048, WIN), ("b", 1536, 1920, WIN), ("b", 1920, 2048, T))
-BANKS = ((0, 4, "s"), (4, 8, "s"), (8, 12, "s"), (12, 14, "s"), (14, 15, "v"), (15, 16, "s"))
+GATHERS = (("w", 0, 1536, WIN), ("b", 0, 1024, WIN), ("b", 1024, 1536, WIN), ("w", 1536, 2048, WIN), ("b", 1536, 1792, WIN), ("b", 1792, 1920, T), ("b", 1920, 2048, T))
+BANKS = ((0, 4, "s"), (4, 8, "s"), (8, 12, "s"), (12, 14, "s"), (14, 15, "s"), (15, 16, "s"))
 PE_ADD = 384
 PE_STEP = 192
 V_CUTS = (384, 640, 896, 1024)

@@ -19,7 +19,7 @@ S = E * C
 FLOPS = 2 * K * N * S
 
 WIN = 2048
-CHUNKS = ((0, 256, 160), (256, 512, 160), (512, 768, 160), (768, 896, 0), (896, 1024, 88))
+CHUNKS = ((0, 512, 352), (512, 768, 160), (768, 896, 0), (896, 1024, 88))
 
 GATHERS = (("w", 0, 1536, WIN), ("b", 0, 1024, WIN), ("b", 1024, 1536, WIN), ("w", 1536, 2048, WIN), ("b", 1536, 1792, WIN), ("b", 1792, 1920, T), ("b", 1920, 2048, T))
 BANKS = ((0, 4, "s"), (4, 8, "s"), (8, 12, "s"), (12, 14, "s"), (14, 15, "s"), (15, 16, "s"))

from contextlib import ExitStack

import concourse.mybir as mybir
from concourse.masks import make_identity

F32 = mybir.dt.float32
BF16 = mybir.dt.bfloat16
I32 = mybir.dt.int32
U32 = mybir.dt.uint32
U16 = mybir.dt.uint16
U8 = mybir.dt.uint8
FP8X4 = mybir.dt.float8_e4m3fn_x4
MULT = mybir.AluOpType.mult
ADD = mybir.AluOpType.add

P = 128
K, T, E, C, N = 512, 1024, 16, 128, 128
S = E * C
FLOPS = 2 * K * N * S

WIN = 2048
CHUNKS = ((0, 512, 352), (512, 768, 160), (768, 896, 0), (896, 1024, 88))

GATHERS = (("w", 0, 1536, WIN), ("b", 0, 1024, WIN), ("b", 1024, 1536, WIN), ("w", 1536, 2048, WIN), ("b", 1536, 1792, WIN), ("b", 1792, 1920, T), ("b", 1920, 2048, T))
BANKS = ((0, 4, "s"), (4, 8, "s"), (8, 12, "s"), (12, 14, "s"), (14, 15, "s"), (15, 16, "s"))
PE_ADD = 384
PE_STEP = 192
V_CUTS = (384, 640, 896, 1024)


def tile_routed_moe_kernel(tc, xT, w_words, w_scales, gate, offs, pos1, pos2, out):
    nc = tc.nc
    with ExitStack() as ctx:
        lists = ctx.enter_context(tc.tile_pool(name="lists", bufs=1))
        keep = ctx.enter_context(tc.tile_pool(name="keep", bufs=1))
        psum = ctx.enter_context(tc.psum_pool(name="psum", bufs=1))

        offs_sb = lists.tile([P, S // 16], U16, name="offs_sb")
        pos1_sb = lists.tile([P, T // 16], U16, name="pos1_sb")
        pos2_sb = lists.tile([P, T // 16], U16, name="pos2_sb")

        warm = keep.tile([P, 8], F32, name="warm")
        warm2 = keep.tile([P, 8], F32, name="warm2")
        nc.vector.memset(warm[:], 0.0)
        nc.scalar.copy(out=warm2[:], in_=warm[:])
        ident = keep.tile([P, P], F32, name="ident")
        make_identity(nc, ident[:])

        tok_words = keep.tile([P, WIN], I32, name="tok_words", align_bytes=64)
        tok_bytes = keep.tile([P, WIN], U8, name="tok_bytes", align_bytes=64)
        nc.vector.memset(tok_words[:, T:WIN], 0)
        nc.vector.memset(tok_bytes[:].bitcast(I32), 0)
        ws = keep.tile([P, E, N], U8, name="ws", align_bytes=64)
        nc.vector.memset(ws[:].bitcast(I32), 0)

        x_view = xT.rearrange("(p j) t -> p j t", j=4)
        raws = []
        for a, b, v in CHUNKS:
            raw = keep.tile([P, 4, b - a], F32, name="raw%d" % a)
            nc.sync.dma_start(out=raw[:], in_=x_view[:, :, a:b])
            raws.append(raw)
        nc.sync.dma_start(offs_sb[:], offs)

        s_view = w_scales.rearrange("e a q n -> q (e a) n")
        for r in range(4):
            nc.sync.dma_start(out=ws[r:P:32, :, :].bitcast(I32), in_=s_view[r:16:4, :, :].bitcast(I32))
        w_sb = keep.tile([P, E, N], I32, name="w_sb", align_bytes=64)
        w_view = w_words.rearrange("e a p n r -> p (e a) (n r)").bitcast(I32)
        for h in range(2):
            nc.sync.dma_start(out=w_sb[:, 8 * h:8 * h + 8, :], in_=w_view[:, 8 * h:8 * h + 8, :])
        nc.sync.dma_start(pos1_sb[:], pos1)
        nc.sync.dma_start(pos2_sb[:], pos2)
        gates = keep.tile([P, 2, T], F32, name="gates")
        nc.sync.dma_start(out=gates[:], in_=gate.rearrange("g p t -> p g t"))
        gate0 = gates[:, 0, :]
        gate1 = gates[:, 1, :]

        for i, (a, b, v) in enumerate(CHUNKS):
            grp = keep.tile([P, b - a, 4], BF16, name="grp%d" % a, align_bytes=64)
            src = raws[i][:].rearrange("p j t -> p t j")
            if v:
                nc.vector.tensor_copy(out=grp[:, 0:v, :], in_=src[:, 0:v, :])
            nc.scalar.copy(out=grp[:, v:b - a, :], in_=src[:, v:b - a, :])
            nc.vector.quantize_mx(
                out=tok_words[:, a:b].bitcast(FP8X4),
                scales=tok_bytes[:, a:b],
                in_=grp[:].rearrange("p t j -> p (t j)"),
            )

        g_words = keep.tile([P, S], U32, name="g_words", align_bytes=64)
        g_bytes = keep.tile([P, S], U8, name="g_bytes", align_bytes=64)
        for sort, a, b, cols in GATHERS:
            lst = offs_sb[:, a // 16:b // 16]
            if sort == "w":
                nc.vector.tensor_copy(out=g_words[:, a:b], in_=tok_words[:, 0:cols].bitcast(U32).indirect(lst))
            else:
                nc.vector.tensor_copy(out=g_bytes[:, a:b], in_=tok_bytes[:, 0:cols].indirect(lst))

        y_sb = keep.tile([P, S], F32, name="y_sb")
        for e0, e1, eng in BANKS:
            acc = psum.tile([P, (e1 - e0) * C], F32, name="acc%d" % e0)
            for e in range(e0, e1):
                nc.tensor.matmul_mx(
                    out=acc[:, (e - e0) * C:(e - e0 + 1) * C],
                    lhsT=w_sb[:, e, :].bitcast(FP8X4),
                    lhsT_scale=ws[:, e, :],
                    rhs=g_words[:, e * C:(e + 1) * C].bitcast(FP8X4),
                    rhs_scale=g_bytes[:, e * C:(e + 1) * C],
                    start=True,
                    stop=True,
                )
            if eng == "v":
                nc.vector.tensor_copy(out=y_sb[:, e0 * C:e1 * C], in_=acc[:])
            else:
                nc.scalar.copy(out=y_sb[:, e0 * C:e1 * C], in_=acc[:])

        part1 = keep.tile([P, T], F32, name="part1")
        part2 = keep.tile([P, T], F32, name="part2")
        res = keep.tile([P, T], F32, name="res")

        def fetch(part, lst, gt, a, b):
            nc.vector.tensor_tensor(out=part[:, a:b], in0=y_sb[:].indirect(lst[:, a // 16:b // 16]), in1=gt[:, a:b], op=MULT)

        def finish(a, b):
            nc.vector.tensor_tensor(out=res[:, a:b], in0=part1[:, a:b], in1=part2[:, a:b], op=ADD)
            nc.sync.dma_start(out=out[:, a:b], in_=res[:, a:b])

        fetch(part1, pos1_sb, gate0, 0, PE_ADD)
        fetch(part2, pos2_sb, gate1, 0, PE_ADD)
        for a in range(0, PE_ADD, PE_STEP):
            b = a + PE_STEP
            total = psum.tile([P, PE_STEP], F32, name="total%d" % a)
            nc.tensor.matmul(total[:], lhsT=ident[:], rhs=part1[:, a:b], start=True, stop=False)
            nc.tensor.matmul(total[:], lhsT=ident[:], rhs=part2[:, a:b], start=False, stop=True)
            nc.scalar.copy(out=res[:, a:b], in_=total[:])
            nc.scalar.dma_start(out=out[:, a:b], in_=res[:, a:b])
        c0, c1, c2, c3 = V_CUTS
        fetch(part1, pos1_sb, gate0, c0, c3)
        fetch(part2, pos2_sb, gate1, c0, c1)
        fetch(part2, pos2_sb, gate1, c1, c2)
        finish(c0, c1)
        fetch(part2, pos2_sb, gate1, c2, c3)
        finish(c1, c2)
        finish(c2, c3)
